import numpy as np, ml_dtypes
CORES = [13,21,141,149]
N = 4
R, NS, T = 4096, 512, 128
def entries(a): return a.T.reshape(-1)
def pack(v, P): return np.ascontiguousarray(np.asarray(v, np.int32).reshape(-1, P).T)
def lists(rng, how):
    I = rng.integers(0, N * R, NS)
    if how == "alike": I[:] = rng.integers(N * R)
    if how == "distinct": I = rng.permutation(N * R)[:NS]
    if how == "hotrank": I = R * int(rng.integers(N)) + rng.integers(0, R, NS)
    if how == "edge": I = R * rng.integers(0, N, NS) + np.where(rng.random(NS) < 0.5, 0, R - 1)
    if how == "sorted": I = np.sort(I)
    return {"neg": np.broadcast_to(pack(I, 16), (N, 16, NS // 16)).copy()}
def setup_inputs(rng):
    return dict({"h": rng.standard_normal((N, 128, T), dtype=np.float32).astype(ml_dtypes.bfloat16), "tab": (rng.standard_normal((N, 128, R), dtype=np.float32) / 8).astype(ml_dtypes.bfloat16)}, **lists(rng, "uniform"))
def setup_inputs_alike(rng):
    d = setup_inputs(rng); d.update(lists(rng, "alike"))
    for k in ("h", "tab"): d[k] = (d[k].astype(np.float32) * 1024.0).astype(d[k].dtype)
    return d
def setup_inputs_distinct(rng):
    d = setup_inputs(rng); d.update(lists(rng, "distinct"))
    for k in ("h", "tab"): d[k] = (d[k].astype(np.float32) * (1 / 1024.0)).astype(d[k].dtype)
    return d
def setup_inputs_edge(rng):
    d = setup_inputs(rng); d.update(lists(rng, "edge"))
    return d
def setup_inputs_hotrank(rng):
    d = setup_inputs(rng); d.update(lists(rng, "hotrank"))
    return d
def setup_inputs_sorted(rng):
    d = setup_inputs(rng); d.update(lists(rng, "sorted"))
    return d
def check_inputs(x):
    bad = []
    if x["neg"].min() < 0 or x["neg"].max() >= N * R: bad.append("neg out of range")
    if not all(np.array_equal(a, x["neg"][0]) for a in x["neg"]): bad.append("neg isn't alike on all ranks")
    return bad
def reference(h, tab, neg):
    A = np.concatenate(list(tab), axis=1).astype(np.float64)
    S = A[:, entries(neg[0])]
    return {"y": np.stack([h[r].astype(np.float64).T @ S for r in range(N)]).astype(ml_dtypes.bfloat16)}

@@ -1,0 +1,143 @@
+from concourse.mybir import AluOpType, ActivationFunctionType
+
+ITEMS, NS, TOK, PAD = 4096, 512, 128, 8
+HALF = NS // 2
+WIN = PAD + ITEMS + PAD
+GROUP, LCOLS = 16, NS // 16
+
+SCRATCH = {
+    "win": ("sbuf", [128, WIN], "bfloat16"),
+    "negs": ("sbuf", [128, LCOLS], "int32"),
+    "off": ("sbuf", [128, LCOLS], "uint16"),
+    "hb": ("sbuf", [128, TOK], "bfloat16"),
+    "mine": ("sbuf", [128, NS], "bfloat16"),
+    "relay": ("sbuf", [128, NS], "bfloat16"),
+    "lp": ("sbuf", [128, NS], "bfloat16"),
+    "la": ("sbuf", [128, NS], "bfloat16"),
+    "lb": ("sbuf", [128, NS], "bfloat16"),
+    "yo": ("sbuf", [128, NS], "bfloat16"),
+    "acc0": ("psum", [128, 512], "float32"),
+    "acc1": ("psum", [128, 512], "float32"),
+}
+SEMAPHORES = ["stab", "sneg", "sh", "spad", "soff", "sg", "sent", "arr", "rp", "ra", "rb", "sm0", "sm1", "sev", "sst"]
+
+
+def _engines(mask):
+    return bin(mask).count("1")
+
+
+def _routes(T, topo):
+    out = {}
+    n = topo.CORES_PER_CHIP
+    for c in T.cores:
+        chipmates = [k for k in range(max(0, c - n + 1), c + n)
+                     if k not in T.cores and topo.host(k) == topo.host(c) and topo.chip(k) == topo.chip(c)]
+        direct = [q for q in T.cores if q != c and topo.may_write(c, q)]
+        far = [q for q in T.cores if q != c and not topo.may_write(c, q)]
+        far.sort(key=lambda q: topo.host(q) != topo.host(c))
+        taken, hops = [], []
+        for q in far:
+            near = topo.host(q) == topo.host(c)
+            cand = [k for k in chipmates if topo.may_write(k, q) and k not in taken]
+            pick = [k for k in cand if (topo.die(k) == topo.die(c)) == near] or cand
+            taken.append(pick[0])
+            hops.append((pick[0], q, "a" if near else "b"))
+        out[c] = (direct, hops)
+    return out
+
+
+def _write(g, topo, src, dst, out_ap, in_ap, remote_sem, local_sem):
+    rid, pid = topo.addr(dst, src)
+    mask = topo.mask(src, dst)
+    g.remote_dma(out_ap=out_ap, in_ap=in_ap, remote_sem=remote_sem, local_sem=local_sem, pid=pid, routing_id=rid,
+                 dma_engine_mask=mask)
+    return _engines(mask)
+
+
+def rank_program(g, core, T, topo):
+    sem = T.sem
+    routes = _routes(T, topo)
+    rank = T.rank_of(core)
+
+    if rank is None:
+        for c in T.cores:
+            for k, q, slot in routes[c][1]:
+                if k == core:
+                    g.wait_ge(sem.arr, _engines(topo.mask(c, k)))
+                    n = _write(g, topo, core, q, T["l" + slot][:, :], T.relay[:, :], sem["r" + slot], sem.sent)
+                    g.wait_ge(sem.sent, n)
+        return
+
+    direct, hops = routes[core]
+    v, s, sy, pe = g.vector, g.scalar, g.sync, g.tensor
+
+    def load_tab(q, p0, p1):
+        q.dma_start(T.win[p0:p1, PAD:PAD + ITEMS], T.tab[p0:p1, :]).then_inc(sem.stab, 16)
+
+    def load_neg(q, grp):
+        q.dma_start(T.negs[GROUP * grp:GROUP * (grp + 1), :], T.neg[:, :]).then_inc(sem.sneg, 16)
+
+    load_tab(sy, 0, 64)
+    load_tab(s, 64, 96)
+    for grp in range(4):
+        load_neg(sy, grp)
+        load_neg(s, 4 + grp)
+    load_tab(s, 96, 128)
+    sy.dma_start(T.hb[:, :], T.h[:, :]).then_inc(sem.sh, 16)
+
+    v.memset(T.win[:, 0:PAD], 0.0).then_inc(sem.spad, 1)
+    v.memset(T.win[:, PAD + ITEMS:WIN], 0.0).then_inc(sem.spad, 1)
+    v.wait_ge(sem.sneg, 128)
+    v.tensor_scalar(out=T.negs[:, :], in0=T.negs[:, :], scalar1=PAD - ITEMS * rank, scalar2=0,
+                    op0=AluOpType.add, op1=AluOpType.max).then_inc(sem.soff, 1)
+    v.wait_ge(sem.soff, 1)
+    v.tensor_scalar(out=T.off[:, :], in0=T.negs[:, :], scalar1=PAD + ITEMS, scalar2=None,
+                    op0=AluOpType.min).then_inc(sem.soff, 1)
+
+    for q in (v, s):
+        q.wait_ge(sem.soff, 2)
+        q.wait_ge(sem.spad, 2)
+        q.wait_ge(sem.stab, 48)
+    v.tensor_copy(out=T.mine[:, 0:HALF], in_=T.win[:, 0:WIN].indirect(T.off[:, 0:LCOLS // 2])).then_inc(sem.sg, 1)
+    s.activation(out=T.mine[:, HALF:NS], in_=T.win[:, 0:WIN].indirect(T.off[:, LCOLS // 2:LCOLS]),
+                 func=ActivationFunctionType.Copy).then_inc(sem.sg, 1)
+
+    g.wait_ge(sem.sg, 2)
+    left = 0
+    for k, q, slot in hops:
+        left += _write(g, topo, core, k, T.relay[:, :], T.mine[:, :], sem.arr, sem.sent)
+    for q in direct:
+        left += _write(g, topo, core, q, T.lp[:, :], T.mine[:, :], sem.rp, sem.sent)
+
+    pe.wait_ge(sem.sh, 16)
+    pe.wait_ge(sem.sg, 2)
+    parts = [(T.mine, None, 0)]
+    for q in direct:
+        parts.append((T.lp, sem.rp, _engines(topo.mask(q, core))))
+    for c in T.cores:
+        for k, q, slot in routes[c][1]:
+            if q == core and slot == "a":
+                parts.append((T.la, sem.ra, _engines(topo.mask(k, core))))
+    for c in T.cores:
+        for k, q, slot in routes[c][1]:
+            if q == core and slot == "b":
+                parts.append((T.lb, sem.rb, _engines(topo.mask(k, core))))
+    for i, (buf, arrived, n) in enumerate(parts):
+        if arrived is not None:
+            pe.wait_ge(arrived, n)
+        first, last = i == 0, i == len(parts) - 1
+        m0 = pe.matmul(T.acc0[:, 0:HALF], T.hb[:, :], buf[:, 0:HALF], first, last)
+        if last:
+            m0.then_inc(sem.sm0, 1)
+        m1 = pe.matmul(T.acc1[:, 0:HALF], T.hb[:, :], buf[:, HALF:NS], first, last)
+        if last:
+            m1.then_inc(sem.sm1, 1)
+
+    v.wait_ge(sem.sm0, 1)
+    v.tensor_copy(out=T.yo[:, 0:HALF], in_=T.acc0[:, 0:HALF]).then_inc(sem.sev, 1)
+    s.wait_ge(sem.sm1, 1)
+    s.activation(out=T.yo[:, HALF:NS], in_=T.acc1[:, 0:HALF], func=ActivationFunctionType.Copy).then_inc(sem.sev, 1)
+    sy.wait_ge(sem.sev, 2)
+    sy.dma_start(T.y[:, :], T.yo[:, :]).then_inc(sem.sst, 16)
+    sy.wait_ge(sem.sst, 16)
+    g.wait_ge(sem.sent, left)

@@ -1,13 +1,16 @@
+from concourse.bass import DstId, RemoteDMATransfer
 from concourse.mybir import AluOpType, ActivationFunctionType
 
 ITEMS, NS, TOK, PAD = 4096, 512, 128, 8
-HALF = NS // 2
 WIN = PAD + ITEMS + PAD
 GROUP, LCOLS = 16, NS // 16
+CH, QU = NS // 2, NS // 4
 
 SCRATCH = {
     "win": ("sbuf", [128, WIN], "bfloat16"),
     "negs": ("sbuf", [128, LCOLS], "int32"),
+    "negf": ("sbuf", [128, LCOLS], "float32"),
+    "rep": ("sbuf", [128, 128], "float32"),
     "off": ("sbuf", [128, LCOLS], "uint16"),
     "hb": ("sbuf", [128, TOK], "bfloat16"),
     "mine": ("sbuf", [128, NS], "bfloat16"),
@@ -18,12 +21,20 @@ SCRATCH = {
     "yo": ("sbuf", [128, NS], "bfloat16"),
     "acc0": ("psum", [128, 512], "float32"),
     "acc1": ("psum", [128, 512], "float32"),
+    "acc2": ("psum", [128, 512], "float32"),
+    "acc3": ("psum", [128, 512], "float32"),
+    "offp": ("psum", [128, 512], "float32"),
 }
-SEMAPHORES = ["stab", "sneg", "sh", "spad", "soff", "sg", "sent", "arr", "rp", "ra", "rb", "sm0", "sm1", "sev", "sst"]
+SEMAPHORES = ["stab", "sneg", "sh", "spad", "sone", "srep", "soff", "scop", "sg0", "sg1", "sent", "arr0", "arr1", "rp",
+              "ra0", "ra1", "rb0", "rb1", "sm0", "sm1", "sm2", "sm3", "sev0", "sev1", "sst"]
+
+
+def _bits(mask):
+    return [e for e in range(mask.bit_length()) if (mask >> e) & 1]
 
 
 def _engines(mask):
-    return bin(mask).count("1")
+    return len(_bits(mask))
 
 
 def _routes(T, topo):
@@ -42,7 +53,11 @@ def _routes(T, topo):
             pick = [k for k in cand if (topo.die(k) == topo.die(c)) == near] or cand
             taken.append(pick[0])
             hops.append((pick[0], q, "a" if near else "b"))
-        out[c] = (direct, hops)
+        shared = []
+        for i, (k, q, slot) in enumerate(hops):
+            mask = sum(1 << e for e in _bits(topo.mask(c, k))[i::len(hops)])
+            shared.append((k, q, slot, mask))
+        out[c] = (direct, shared)
     return out
 
 
@@ -61,83 +76,108 @@ def rank_program(g, core, T, topo):
 
     if rank is None:
         for c in T.cores:
-            for k, q, slot in routes[c][1]:
+            for k, q, slot, mask in routes[c][1]:
                 if k == core:
-                    g.wait_ge(sem.arr, _engines(topo.mask(c, k)))
-                    n = _write(g, topo, core, q, T["l" + slot][:, :], T.relay[:, :], sem["r" + slot], sem.sent)
-                    g.wait_ge(sem.sent, n)
+                    left = 0
+                    for ch in range(2):
+                        cols = slice(CH * ch, CH * (ch + 1))
+                        g.wait_ge(sem["arr%d" % ch], _engines(mask))
+                        left += _write(g, topo, core, q, T["l" + slot][:, cols], T.relay[:, cols],
+                                       sem["r%s%d" % (slot, ch)], sem.sent)
+                    g.wait_ge(sem.sent, left)
         return
 
     direct, hops = routes[core]
     v, s, sy, pe = g.vector, g.scalar, g.sync, g.tensor
+    copy = ActivationFunctionType.Copy
 
     def load_tab(q, p0, p1):
         q.dma_start(T.win[p0:p1, PAD:PAD + ITEMS], T.tab[p0:p1, :]).then_inc(sem.stab, 16)
 
-    def load_neg(q, grp):
-        q.dma_start(T.negs[GROUP * grp:GROUP * (grp + 1), :], T.neg[:, :]).then_inc(sem.sneg, 16)
-
-    load_tab(sy, 0, 64)
-    load_tab(s, 64, 96)
-    for grp in range(4):
-        load_neg(sy, grp)
-        load_neg(s, 4 + grp)
+    sy.dma_start(T.negs[0:GROUP, :], T.neg[:, :]).then_inc(sem.sneg, 16)
+    load_tab(s, 32, 64)
+    load_tab(sy, 0, 32)
     load_tab(s, 96, 128)
+    load_tab(sy, 64, 96)
     sy.dma_start(T.hb[:, :], T.h[:, :]).then_inc(sem.sh, 16)
 
+    v.memset(T.rep[0:GROUP, :], 1.0).then_inc(sem.sone, 1)
     v.memset(T.win[:, 0:PAD], 0.0).then_inc(sem.spad, 1)
     v.memset(T.win[:, PAD + ITEMS:WIN], 0.0).then_inc(sem.spad, 1)
-    v.wait_ge(sem.sneg, 128)
-    v.tensor_scalar(out=T.negs[:, :], in0=T.negs[:, :], scalar1=PAD - ITEMS * rank, scalar2=0,
+    g.wait_ge(sem.sone, 1)
+    g.affine_select(out=T.rep[0:GROUP, :], in_=T.rep[0:GROUP, :], pattern=[[0, 128 // GROUP], [-1, GROUP]],
+                    compare_op=AluOpType.is_equal, fill=0.0, base=0, channel_multiplier=1).then_inc(sem.srep, 1)
+    v.wait_ge(sem.sneg, 16)
+    v.tensor_scalar(out=T.negf[0:GROUP, :], in0=T.negs[0:GROUP, :], scalar1=PAD - ITEMS * rank, scalar2=0,
                     op0=AluOpType.add, op1=AluOpType.max).then_inc(sem.soff, 1)
-    v.wait_ge(sem.soff, 1)
-    v.tensor_scalar(out=T.off[:, :], in0=T.negs[:, :], scalar1=PAD + ITEMS, scalar2=None,
+    pe.wait_ge(sem.srep, 1)
+    pe.wait_ge(sem.soff, 1)
+    pe.matmul(T.offp[:, 0:LCOLS], T.rep[0:GROUP, :], T.negf[0:GROUP, :], True, True).then_inc(sem.scop, 1)
+    v.wait_ge(sem.scop, 1)
+    v.tensor_scalar(out=T.off[:, :], in0=T.offp[:, 0:LCOLS], scalar1=PAD + ITEMS, scalar2=None,
                     op0=AluOpType.min).then_inc(sem.soff, 1)
 
     for q in (v, s):
         q.wait_ge(sem.soff, 2)
         q.wait_ge(sem.spad, 2)
-        q.wait_ge(sem.stab, 48)
-    v.tensor_copy(out=T.mine[:, 0:HALF], in_=T.win[:, 0:WIN].indirect(T.off[:, 0:LCOLS // 2])).then_inc(sem.sg, 1)
-    s.activation(out=T.mine[:, HALF:NS], in_=T.win[:, 0:WIN].indirect(T.off[:, LCOLS // 2:LCOLS]),
-                 func=ActivationFunctionType.Copy).then_inc(sem.sg, 1)
+        q.wait_ge(sem.stab, 64)
+    lq = LCOLS // 4
+    for ch in range(2):
+        q0, q1 = 2 * ch, 2 * ch + 1
+        v.tensor_copy(out=T.mine[:, QU * q0:QU * (q0 + 1)],
+                      in_=T.win[:, 0:WIN].indirect(T.off[:, lq * q0:lq * (q0 + 1)])).then_inc(sem["sg%d" % ch], 1)
+        s.activation(out=T.mine[:, QU * q1:QU * (q1 + 1)],
+                     in_=T.win[:, 0:WIN].indirect(T.off[:, lq * q1:lq * (q1 + 1)]), func=copy).then_inc(sem["sg%d" % ch], 1)
 
-    g.wait_ge(sem.sg, 2)
     left = 0
-    for k, q, slot in hops:
-        left += _write(g, topo, core, k, T.relay[:, :], T.mine[:, :], sem.arr, sem.sent)
+    for ch in range(2):
+        cols = slice(CH * ch, CH * (ch + 1))
+        g.wait_ge(sem["sg%d" % ch], 2)
+        transfers = []
+        for k, q, slot, mask in hops:
+            rid, pid = topo.addr(k, core)
+            transfers.append(RemoteDMATransfer(dst_ids=[DstId(rid=rid, pnc=pid)], dma_engine_mask=mask,
+                                               remote_sem=sem["arr%d" % ch], src=T.mine[:, cols], dst=T.relay[:, cols]))
+            left += _engines(mask)
+        g.remote_dma_fused(transfers, local_sem=sem.sent)
     for q in direct:
         left += _write(g, topo, core, q, T.lp[:, :], T.mine[:, :], sem.rp, sem.sent)
 
-    pe.wait_ge(sem.sh, 16)
-    pe.wait_ge(sem.sg, 2)
-    parts = [(T.mine, None, 0)]
-    for q in direct:
-        parts.append((T.lp, sem.rp, _engines(topo.mask(q, core))))
-    for c in T.cores:
-        for k, q, slot in routes[c][1]:
-            if q == core and slot == "a":
-                parts.append((T.la, sem.ra, _engines(topo.mask(k, core))))
-    for c in T.cores:
-        for k, q, slot in routes[c][1]:
-            if q == core and slot == "b":
-                parts.append((T.lb, sem.rb, _engines(topo.mask(k, core))))
-    for i, (buf, arrived, n) in enumerate(parts):
-        if arrived is not None:
-            pe.wait_ge(arrived, n)
-        first, last = i == 0, i == len(parts) - 1
-        m0 = pe.matmul(T.acc0[:, 0:HALF], T.hb[:, :], buf[:, 0:HALF], first, last)
+    def mm(buf, qu, first, last):
+        m = pe.matmul(T["acc%d" % qu][:, 0:QU], T.hb[:, :], buf[:, QU * qu:QU * (qu + 1)], first, last)
         if last:
-            m0.then_inc(sem.sm0, 1)
-        m1 = pe.matmul(T.acc1[:, 0:HALF], T.hb[:, :], buf[:, HALF:NS], first, last)
-        if last:
-            m1.then_inc(sem.sm1, 1)
+            m.then_inc(sem["sm%d" % qu], 1)
 
-    v.wait_ge(sem.sm0, 1)
-    v.tensor_copy(out=T.yo[:, 0:HALF], in_=T.acc0[:, 0:HALF]).then_inc(sem.sev, 1)
-    s.wait_ge(sem.sm1, 1)
-    s.activation(out=T.yo[:, HALF:NS], in_=T.acc1[:, 0:HALF], func=ActivationFunctionType.Copy).then_inc(sem.sev, 1)
-    sy.wait_ge(sem.sev, 2)
-    sy.dma_start(T.y[:, :], T.yo[:, :]).then_inc(sem.sst, 16)
-    sy.wait_ge(sem.sst, 16)
+    came = {}
+    for c in T.cores:
+        for k, q, slot, mask in routes[c][1]:
+            if q == core:
+                came[slot] = _engines(topo.mask(k, core))
+    pe.wait_ge(sem.sh, 16)
+    for ch in range(2):
+        pe.wait_ge(sem["sg%d" % ch], 2)
+        mm(T.mine, 2 * ch, True, False)
+        mm(T.mine, 2 * ch + 1, True, False)
+    for q in direct:
+        pe.wait_ge(sem.rp, _engines(topo.mask(q, core)))
+        for qu in range(4):
+            mm(T.lp, qu, False, False)
+    slots = sorted(came)
+    for ch in range(2):
+        for slot in slots:
+            pe.wait_ge(sem["r%s%d" % (slot, ch)], came[slot])
+            mm(T["l" + slot], 2 * ch, False, slot == slots[-1])
+            mm(T["l" + slot], 2 * ch + 1, False, slot == slots[-1])
+
+    for ch in range(2):
+        q0, q1 = 2 * ch, 2 * ch + 1
+        v.wait_ge(sem["sm%d" % q0], 1)
+        v.tensor_copy(out=T.yo[:, QU * q0:QU * (q0 + 1)], in_=T["acc%d" % q0][:, 0:QU]).then_inc(sem["sev%d" % ch], 1)
+        s.wait_ge(sem["sm%d" % q1], 1)
+        s.activation(out=T.yo[:, QU * q1:QU * (q1 + 1)], in_=T["acc%d" % q1][:, 0:QU],
+                     func=copy).then_inc(sem["sev%d" % ch], 1)
+        cols = slice(CH * ch, CH * (ch + 1))
+        sy.wait_ge(sem["sev%d" % ch], 2)
+        sy.dma_start(T.y[:, cols], T.yo[:, cols]).then_inc(sem.sst, 16)
+    sy.wait_ge(sem.sst, 32)
     g.wait_ge(sem.sent, left)

@@ -5,15 +5,19 @@ ITEMS, NS, TOK, PAD = 4096, 512, 128, 8
 WIN = PAD + ITEMS + PAD
 GROUP, LCOLS = 16, NS // 16
 CH, QU = NS // 2, NS // 4
+RAW = 3 * QU
 
 SCRATCH = {
     "win": ("sbuf", [128, WIN], "bfloat16"),
     "negs": ("sbuf", [128, LCOLS], "int32"),
     "negf": ("sbuf", [128, LCOLS], "float32"),
     "rep": ("sbuf", [128, 128], "float32"),
+    "ident": ("sbuf", [128, 128], "bfloat16"),
     "off": ("sbuf", [128, LCOLS], "uint16"),
     "hb": ("sbuf", [128, TOK], "bfloat16"),
+    "hp": ("sbuf", [128, TOK], "bfloat16"),
     "mine": ("sbuf", [128, NS], "bfloat16"),
+    "pb": ("sbuf", [128, QU], "bfloat16"),
     "relay": ("sbuf", [128, NS], "bfloat16"),
     "lp": ("sbuf", [128, NS], "bfloat16"),
     "la": ("sbuf", [128, NS], "bfloat16"),
@@ -23,10 +27,11 @@ SCRATCH = {
     "acc1": ("psum", [128, 512], "float32"),
     "acc2": ("psum", [128, 512], "float32"),
     "acc3": ("psum", [128, 512], "float32"),
+    "pacc": ("psum", [128, 512], "float32"),
     "offp": ("psum", [128, 512], "float32"),
 }
-SEMAPHORES = ["stab", "sneg", "sh", "spad", "sone", "srep", "soff", "scop", "sg0", "sg1", "sent", "arr0", "arr1", "rp",
-              "ra0", "ra1", "rb0", "rb1", "sm0", "sm1", "sm2", "sm3", "sev0", "sev1", "sst"]
+SEMAPHORES = ["stab", "sneg", "sh", "spad", "sone", "srep", "sid", "soff", "scop", "sg0", "sg1", "sent", "arr0", "arr1",
+              "rh", "rp", "rs", "ra0", "ra1", "rb0", "rb1", "sp", "spv", "sm0", "sm1", "sm2", "sm3", "sev0", "sev1", "sst"]
 
 
 def _bits(mask):
@@ -88,6 +93,8 @@ def rank_program(g, core, T, topo):
         return
 
     direct, hops = routes[core]
+    partner = direct[0]
+    from_partner = _engines(topo.mask(partner, core))
     v, s, sy, pe = g.vector, g.scalar, g.sync, g.tensor
     copy = ActivationFunctionType.Copy
 
@@ -95,18 +102,24 @@ def rank_program(g, core, T, topo):
         q.dma_start(T.win[p0:p1, PAD:PAD + ITEMS], T.tab[p0:p1, :]).then_inc(sem.stab, 16)
 
     sy.dma_start(T.negs[0:GROUP, :], T.neg[:, :]).then_inc(sem.sneg, 16)
+    s.dma_start(T.hb[:, :], T.h[:, :]).then_inc(sem.sh, 16)
     load_tab(s, 32, 64)
     load_tab(sy, 0, 32)
     load_tab(s, 96, 128)
     load_tab(sy, 64, 96)
-    sy.dma_start(T.hb[:, :], T.h[:, :]).then_inc(sem.sh, 16)
 
     v.memset(T.rep[0:GROUP, :], 1.0).then_inc(sem.sone, 1)
+    v.memset(T.ident[:, :], 1.0).then_inc(sem.sone, 1)
     v.memset(T.win[:, 0:PAD], 0.0).then_inc(sem.spad, 1)
     v.memset(T.win[:, PAD + ITEMS:WIN], 0.0).then_inc(sem.spad, 1)
-    g.wait_ge(sem.sone, 1)
+    g.wait_ge(sem.sone, 2)
     g.affine_select(out=T.rep[0:GROUP, :], in_=T.rep[0:GROUP, :], pattern=[[0, 128 // GROUP], [-1, GROUP]],
                     compare_op=AluOpType.is_equal, fill=0.0, base=0, channel_multiplier=1).then_inc(sem.srep, 1)
+    g.affine_select(out=T.ident[:, :], in_=T.ident[:, :], pattern=[[-1, 128]],
+                    compare_op=AluOpType.is_equal, fill=0.0, base=0, channel_multiplier=1).then_inc(sem.sid, 1)
+    g.wait_ge(sem.sh, 16)
+    left = _write(g, topo, core, partner, T.hp[:, :], T.hb[:, :], sem.rh, sem.sent)
+
     v.wait_ge(sem.sneg, 16)
     v.tensor_scalar(out=T.negf[0:GROUP, :], in0=T.negs[0:GROUP, :], scalar1=PAD - ITEMS * rank, scalar2=0,
                     op0=AluOpType.add, op1=AluOpType.max).then_inc(sem.soff, 1)
@@ -129,7 +142,6 @@ def rank_program(g, core, T, topo):
         s.activation(out=T.mine[:, QU * q1:QU * (q1 + 1)],
                      in_=T.win[:, 0:WIN].indirect(T.off[:, lq * q1:lq * (q1 + 1)]), func=copy).then_inc(sem["sg%d" % ch], 1)
 
-    left = 0
     for ch in range(2):
         cols = slice(CH * ch, CH * (ch + 1))
         g.wait_ge(sem["sg%d" % ch], 2)
@@ -140,11 +152,12 @@ def rank_program(g, core, T, topo):
                                                remote_sem=sem["arr%d" % ch], src=T.mine[:, cols], dst=T.relay[:, cols]))
             left += _engines(mask)
         g.remote_dma_fused(transfers, local_sem=sem.sent)
-    for q in direct:
-        left += _write(g, topo, core, q, T.lp[:, :], T.mine[:, :], sem.rp, sem.sent)
+    left += _write(g, topo, core, partner, T.lp[:, 0:RAW], T.mine[:, 0:RAW], sem.rp, sem.sent)
+    g.wait_ge(sem.spv, 1)
+    left += _write(g, topo, core, partner, T.lp[:, RAW:NS], T.pb[:, :], sem.rs, sem.sent)
 
-    def mm(buf, qu, first, last):
-        m = pe.matmul(T["acc%d" % qu][:, 0:QU], T.hb[:, :], buf[:, QU * qu:QU * (qu + 1)], first, last)
+    def mm(lhsT, buf, qu, first, last):
+        m = pe.matmul(T["acc%d" % qu][:, 0:QU], lhsT[:, :], buf[:, QU * qu:QU * (qu + 1)], first, last)
         if last:
             m.then_inc(sem["sm%d" % qu], 1)
 
@@ -153,21 +166,32 @@ def rank_program(g, core, T, topo):
         for k, q, slot, mask in routes[c][1]:
             if q == core:
                 came[slot] = _engines(topo.mask(k, core))
+    slots = sorted(came)
+
+    def relayed(ch):
+        for slot in slots:
+            pe.wait_ge(sem["r%s%d" % (slot, ch)], came[slot])
+            mm(T.hb, T["l" + slot], 2 * ch, False, slot == slots[-1])
+            mm(T.hb, T["l" + slot], 2 * ch + 1, False, slot == slots[-1])
+
     pe.wait_ge(sem.sh, 16)
     for ch in range(2):
         pe.wait_ge(sem["sg%d" % ch], 2)
-        mm(T.mine, 2 * ch, True, False)
-        mm(T.mine, 2 * ch + 1, True, False)
-    for q in direct:
-        pe.wait_ge(sem.rp, _engines(topo.mask(q, core)))
-        for qu in range(4):
-            mm(T.lp, qu, False, False)
-    slots = sorted(came)
-    for ch in range(2):
-        for slot in slots:
-            pe.wait_ge(sem["r%s%d" % (slot, ch)], came[slot])
-            mm(T["l" + slot], 2 * ch, False, slot == slots[-1])
-            mm(T["l" + slot], 2 * ch + 1, False, slot == slots[-1])
+        mm(T.hb, T.mine, 2 * ch, True, False)
+        mm(T.hb, T.mine, 2 * ch + 1, True, False)
+    pe.wait_ge(sem.rh, from_partner)
+    pe.matmul(T.pacc[:, 0:QU], T.hp[:, :], T.mine[:, RAW:NS], True, True).then_inc(sem.sp, 1)
+    pe.wait_ge(sem.rp, from_partner)
+    for qu in range(RAW // QU):
+        mm(T.hb, T.lp, qu, False, False)
+    relayed(0)
+    pe.wait_ge(sem.sid, 1)
+    pe.wait_ge(sem.rs, from_partner)
+    mm(T.ident, T.lp, RAW // QU, False, False)
+    relayed(1)
+
+    v.wait_ge(sem.sp, 1)
+    v.tensor_copy(out=T.pb[:, :], in_=T.pacc[:, 0:QU]).then_inc(sem.spv, 1)
 
     for ch in range(2):
         q0, q1 = 2 * ch, 2 * ch + 1

@@ -4,8 +4,10 @@ from concourse.mybir import AluOpType, ActivationFunctionType
 ITEMS, NS, TOK, PAD = 4096, 512, 128, 8
 WIN = PAD + ITEMS + PAD
 GROUP, LCOLS = 16, NS // 16
-CH, QU = NS // 2, NS // 4
-RAW = 3 * QU
+NQ = 4
+CH, QU = NS // 2, NS // NQ
+QRAW, QSC = 0, 1
+IDW = 32
 
 SCRATCH = {
     "win": ("sbuf", [128, WIN], "bfloat16"),
@@ -13,12 +15,13 @@ SCRATCH = {
     "negf": ("sbuf", [128, LCOLS], "float32"),
     "rep": ("sbuf", [128, 128], "float32"),
     "ident": ("sbuf", [128, 128], "bfloat16"),
+    "idq": ("sbuf", [128, IDW], "bfloat16"),
     "off": ("sbuf", [128, LCOLS], "uint16"),
     "hb": ("sbuf", [128, TOK], "bfloat16"),
     "hp": ("sbuf", [128, TOK], "bfloat16"),
     "mine": ("sbuf", [128, NS], "bfloat16"),
     "pb": ("sbuf", [128, QU], "bfloat16"),
-    "relay": ("sbuf", [128, NS], "bfloat16"),
+    "relay": ("sbuf", [128, QU], "bfloat16"),
     "lp": ("sbuf", [128, NS], "bfloat16"),
     "la": ("sbuf", [128, NS], "bfloat16"),
     "lb": ("sbuf", [128, NS], "bfloat16"),
@@ -30,8 +33,8 @@ SCRATCH = {
     "pacc": ("psum", [128, 512], "float32"),
     "offp": ("psum", [128, 512], "float32"),
 }
-SEMAPHORES = ["stab", "sneg", "sh", "spad", "sone", "srep", "sid", "soff", "scop", "sg0", "sg1", "sent", "arr0", "arr1",
-              "rh", "rp", "rs", "ra0", "ra1", "rb0", "rb1", "sp", "spv", "sm0", "sm1", "sm2", "sm3", "sev0", "sev1", "sst"]
+SEMAPHORES = ["stab", "sneg", "sh", "spad", "sone", "srep", "sid", "soff", "scop", "sg0", "sg1", "sent", "arr",
+              "rh", "rp", "rs", "rq0", "rq1", "rq2", "rq3", "sp", "spv", "sm0", "sm1", "sm2", "sm3", "sev0", "sev1", "sst"]
 
 
 def _bits(mask):
@@ -40,6 +43,10 @@ def _bits(mask):
 
 def _engines(mask):
     return len(_bits(mask))
+
+
+def _pick(mask, i, n):
+    return sum(1 << e for e in _bits(mask)[i::n])
 
 
 def _routes(T, topo):
@@ -51,24 +58,29 @@ def _routes(T, topo):
         direct = [q for q in T.cores if q != c and topo.may_write(c, q)]
         far = [q for q in T.cores if q != c and not topo.may_write(c, q)]
         far.sort(key=lambda q: topo.host(q) != topo.host(c))
-        taken, hops = [], []
-        for q in far:
-            near = topo.host(q) == topo.host(c)
-            cand = [k for k in chipmates if topo.may_write(k, q) and k not in taken]
-            pick = [k for k in cand if (topo.die(k) == topo.die(c)) == near] or cand
-            taken.append(pick[0])
-            hops.append((pick[0], q, "a" if near else "b"))
-        shared = []
-        for i, (k, q, slot) in enumerate(hops):
-            mask = sum(1 << e for e in _bits(topo.mask(c, k))[i::len(hops)])
-            shared.append((k, q, slot, mask))
-        out[c] = (direct, shared)
+
+        def in_turn(cores):
+            same = [k for k in cores if topo.die(k) == topo.die(c)]
+            other = [k for k in cores if topo.die(k) != topo.die(c)]
+            return [k for pair in zip(same, other) for k in pair]
+
+        ported = in_turn([k for k in chipmates if all(topo.may_write(k, q) for q in far)])[:NQ]
+        spare = in_turn([k for k in chipmates if k not in ported and topo.may_write(k, direct[0])])[:2]
+        carriers = []
+        for qu, k in enumerate(ported):
+            legs = [(q, "a" if topo.host(q) == topo.host(c) else "b", _pick(topo.mask(k, q), j, len(far)))
+                    for j, q in enumerate(far)]
+            carriers.append((k, qu, _pick(topo.mask(c, k), qu % 2, 2), legs))
+        for i, k in enumerate(spare):
+            carriers.append((k, NQ - 2 + i, _pick(topo.mask(c, k), i, 2), [(direct[0], "p", topo.mask(k, direct[0]))]))
+        out[c] = (direct, carriers)
     return out
 
 
-def _write(g, topo, src, dst, out_ap, in_ap, remote_sem, local_sem):
+def _write(g, topo, src, dst, out_ap, in_ap, remote_sem, local_sem, mask=None):
     rid, pid = topo.addr(dst, src)
-    mask = topo.mask(src, dst)
+    if mask is None:
+        mask = topo.mask(src, dst)
     g.remote_dma(out_ap=out_ap, in_ap=in_ap, remote_sem=remote_sem, local_sem=local_sem, pid=pid, routing_id=rid,
                  dma_engine_mask=mask)
     return _engines(mask)
@@ -81,22 +93,40 @@ def rank_program(g, core, T, topo):
 
     if rank is None:
         for c in T.cores:
-            for k, q, slot, mask in routes[c][1]:
-                if k == core:
-                    left = 0
-                    for ch in range(2):
-                        cols = slice(CH * ch, CH * (ch + 1))
-                        g.wait_ge(sem["arr%d" % ch], _engines(mask))
-                        left += _write(g, topo, core, q, T["l" + slot][:, cols], T.relay[:, cols],
-                                       sem["r%s%d" % (slot, ch)], sem.sent)
-                    g.wait_ge(sem.sent, left)
+            carriers = routes[c][1]
+            for i, (k, qu, on, legs) in enumerate(carriers):
+                if k != core:
+                    continue
+                lo, hi = TOK * i // len(carriers), TOK * (i + 1) // len(carriers)
+                g.vector.memset(T.idq[:, 0:hi - lo], 1.0).then_inc(sem.sone, 1)
+                g.wait_ge(sem.sone, 1)
+                g.affine_select(out=T.idq[:, 0:hi - lo], in_=T.idq[:, 0:hi - lo], pattern=[[-1, hi - lo]],
+                                compare_op=AluOpType.is_equal, fill=0.0, base=-lo, channel_multiplier=1).then_inc(sem.srep, 1)
+                g.wait_ge(sem.srep, 1)
+                later = 0
+                for q, slot, off in legs:
+                    later |= off
+                left = _write(g, topo, core, c, T.ident[:, lo:hi], T.idq[:, 0:hi - lo], sem.sid, sem.sent, later)
+                g.wait_ge(sem.arr, _engines(on))
+                transfers = []
+                for q, slot, off in legs:
+                    rid, pid = topo.addr(q, core)
+                    transfers.append(RemoteDMATransfer(dst_ids=[DstId(rid=rid, pnc=pid)], dma_engine_mask=off,
+                                                       remote_sem=sem["rq%d" % qu], src=T.relay[:, :],
+                                                       dst=T["l" + slot][:, QU * qu:QU * (qu + 1)]))
+                    left += _engines(off)
+                g.remote_dma_fused(transfers, local_sem=sem.sent)
+                g.wait_ge(sem.sent, left)
         return
 
-    direct, hops = routes[core]
+    direct, carriers = routes[core]
     partner = direct[0]
     from_partner = _engines(topo.mask(partner, core))
     v, s, sy, pe = g.vector, g.scalar, g.sync, g.tensor
     copy = ActivationFunctionType.Copy
+
+    def quarter(qu):
+        return slice(QU * qu, QU * (qu + 1))
 
     def load_tab(q, p0, p1):
         q.dma_start(T.win[p0:p1, PAD:PAD + ITEMS], T.tab[p0:p1, :]).then_inc(sem.stab, 16)
@@ -109,14 +139,11 @@ def rank_program(g, core, T, topo):
     load_tab(sy, 64, 96)
 
     v.memset(T.rep[0:GROUP, :], 1.0).then_inc(sem.sone, 1)
-    v.memset(T.ident[:, :], 1.0).then_inc(sem.sone, 1)
     v.memset(T.win[:, 0:PAD], 0.0).then_inc(sem.spad, 1)
     v.memset(T.win[:, PAD + ITEMS:WIN], 0.0).then_inc(sem.spad, 1)
-    g.wait_ge(sem.sone, 2)
+    g.wait_ge(sem.sone, 1)
     g.affine_select(out=T.rep[0:GROUP, :], in_=T.rep[0:GROUP, :], pattern=[[0, 128 // GROUP], [-1, GROUP]],
                     compare_op=AluOpType.is_equal, fill=0.0, base=0, channel_multiplier=1).then_inc(sem.srep, 1)
-    g.affine_select(out=T.ident[:, :], in_=T.ident[:, :], pattern=[[-1, 128]],
-                    compare_op=AluOpType.is_equal, fill=0.0, base=0, channel_multiplier=1).then_inc(sem.sid, 1)
     g.wait_ge(sem.sh, 16)
     left = _write(g, topo, core, partner, T.hp[:, :], T.hb[:, :], sem.rh, sem.sent)
 
@@ -134,61 +161,69 @@ def rank_program(g, core, T, topo):
         q.wait_ge(sem.soff, 2)
         q.wait_ge(sem.spad, 2)
         q.wait_ge(sem.stab, 64)
-    lq = LCOLS // 4
+    lq = LCOLS // NQ
     for ch in range(2):
         q0, q1 = 2 * ch, 2 * ch + 1
-        v.tensor_copy(out=T.mine[:, QU * q0:QU * (q0 + 1)],
+        v.tensor_copy(out=T.mine[:, quarter(q0)],
                       in_=T.win[:, 0:WIN].indirect(T.off[:, lq * q0:lq * (q0 + 1)])).then_inc(sem["sg%d" % ch], 1)
-        s.activation(out=T.mine[:, QU * q1:QU * (q1 + 1)],
+        s.activation(out=T.mine[:, quarter(q1)],
                      in_=T.win[:, 0:WIN].indirect(T.off[:, lq * q1:lq * (q1 + 1)]), func=copy).then_inc(sem["sg%d" % ch], 1)
 
-    for ch in range(2):
-        cols = slice(CH * ch, CH * (ch + 1))
-        g.wait_ge(sem["sg%d" % ch], 2)
+    seen = -1
+    for i in range(0, len(carriers), 2):
         transfers = []
-        for k, q, slot, mask in hops:
+        for k, qu, on, legs in carriers[i:i + 2]:
+            while seen < qu // 2:
+                seen += 1
+                g.wait_ge(sem["sg%d" % seen], 2)
             rid, pid = topo.addr(k, core)
-            transfers.append(RemoteDMATransfer(dst_ids=[DstId(rid=rid, pnc=pid)], dma_engine_mask=mask,
-                                               remote_sem=sem["arr%d" % ch], src=T.mine[:, cols], dst=T.relay[:, cols]))
-            left += _engines(mask)
+            transfers.append(RemoteDMATransfer(dst_ids=[DstId(rid=rid, pnc=pid)], dma_engine_mask=on, remote_sem=sem.arr,
+                                               src=T.mine[:, quarter(qu)], dst=T.relay[:, :]))
+            left += _engines(on)
         g.remote_dma_fused(transfers, local_sem=sem.sent)
-    left += _write(g, topo, core, partner, T.lp[:, 0:RAW], T.mine[:, 0:RAW], sem.rp, sem.sent)
+    left += _write(g, topo, core, partner, T.lp[:, quarter(QRAW)], T.mine[:, quarter(QRAW)], sem.rp, sem.sent)
     g.wait_ge(sem.spv, 1)
-    left += _write(g, topo, core, partner, T.lp[:, RAW:NS], T.pb[:, :], sem.rs, sem.sent)
+    left += _write(g, topo, core, partner, T.lp[:, quarter(QSC)], T.pb[:, :], sem.rs, sem.sent)
 
     def mm(lhsT, buf, qu, first, last):
-        m = pe.matmul(T["acc%d" % qu][:, 0:QU], lhsT[:, :], buf[:, QU * qu:QU * (qu + 1)], first, last)
+        m = pe.matmul(T["acc%d" % qu][:, 0:QU], lhsT[:, :], buf[:, quarter(qu)], first, last)
         if last:
             m.then_inc(sem["sm%d" % qu], 1)
 
-    came = {}
+    came = {qu: [] for qu in range(NQ)}
+    ident_in = 0
     for c in T.cores:
-        for k, q, slot, mask in routes[c][1]:
-            if q == core:
-                came[slot] = _engines(topo.mask(k, core))
-    slots = sorted(came)
+        for k, qu, on, legs in routes[c][1]:
+            for q, slot, off in legs:
+                if q == core:
+                    came[qu].append((slot, _engines(off)))
+                if c == core:
+                    ident_in += _engines(off)
 
-    def relayed(ch):
+    def carried(qu):
+        pe.wait_ge(sem["rq%d" % qu], sum(n for slot, n in came[qu]))
+        slots = sorted(slot for slot, n in came[qu])
         for slot in slots:
-            pe.wait_ge(sem["r%s%d" % (slot, ch)], came[slot])
-            mm(T.hb, T["l" + slot], 2 * ch, False, slot == slots[-1])
-            mm(T.hb, T["l" + slot], 2 * ch + 1, False, slot == slots[-1])
+            mm(T.hb, T["l" + slot], qu, False, slot == slots[-1])
 
     pe.wait_ge(sem.sh, 16)
-    for ch in range(2):
-        pe.wait_ge(sem["sg%d" % ch], 2)
-        mm(T.hb, T.mine, 2 * ch, True, False)
-        mm(T.hb, T.mine, 2 * ch + 1, True, False)
+    pe.wait_ge(sem.sg0, 2)
+    mm(T.hb, T.mine, 0, True, False)
+    mm(T.hb, T.mine, 1, True, False)
     pe.wait_ge(sem.rh, from_partner)
-    pe.matmul(T.pacc[:, 0:QU], T.hp[:, :], T.mine[:, RAW:NS], True, True).then_inc(sem.sp, 1)
+    pe.matmul(T.pacc[:, 0:QU], T.hp[:, :], T.mine[:, quarter(QSC)], True, True).then_inc(sem.sp, 1)
+    pe.wait_ge(sem.sg1, 2)
+    mm(T.hb, T.mine, 2, True, False)
+    mm(T.hb, T.mine, 3, True, False)
     pe.wait_ge(sem.rp, from_partner)
-    for qu in range(RAW // QU):
-        mm(T.hb, T.lp, qu, False, False)
-    relayed(0)
-    pe.wait_ge(sem.sid, 1)
+    mm(T.hb, T.lp, QRAW, False, False)
+    carried(QRAW)
+    pe.wait_ge(sem.sid, ident_in)
     pe.wait_ge(sem.rs, from_partner)
-    mm(T.ident, T.lp, RAW // QU, False, False)
-    relayed(1)
+    mm(T.ident, T.lp, QSC, False, False)
+    carried(QSC)
+    carried(2)
+    carried(3)
 
     v.wait_ge(sem.sp, 1)
     v.tensor_copy(out=T.pb[:, :], in_=T.pacc[:, 0:QU]).then_inc(sem.spv, 1)
@@ -196,9 +231,9 @@ def rank_program(g, core, T, topo):
     for ch in range(2):
         q0, q1 = 2 * ch, 2 * ch + 1
         v.wait_ge(sem["sm%d" % q0], 1)
-        v.tensor_copy(out=T.yo[:, QU * q0:QU * (q0 + 1)], in_=T["acc%d" % q0][:, 0:QU]).then_inc(sem["sev%d" % ch], 1)
+        v.tensor_copy(out=T.yo[:, quarter(q0)], in_=T["acc%d" % q0][:, 0:QU]).then_inc(sem["sev%d" % ch], 1)
         s.wait_ge(sem["sm%d" % q1], 1)
-        s.activation(out=T.yo[:, QU * q1:QU * (q1 + 1)], in_=T["acc%d" % q1][:, 0:QU],
+        s.activation(out=T.yo[:, quarter(q1)], in_=T["acc%d" % q1][:, 0:QU],
                      func=copy).then_inc(sem["sev%d" % ch], 1)
         cols = slice(CH * ch, CH * (ch + 1))
         sy.wait_ge(sem["sev%d" % ch], 2)

from concourse.bass import DstId, RemoteDMATransfer
from concourse.mybir import AluOpType, ActivationFunctionType

ITEMS, NS, TOK, PAD = 4096, 512, 128, 8
WIN = PAD + ITEMS + PAD
GROUP, LCOLS = 16, NS // 16
NQ = 4
CH, QU = NS // 2, NS // NQ
QRAW, QSC = 0, 1
IDW = 32

SCRATCH = {
    "win": ("sbuf", [128, WIN], "bfloat16"),
    "negs": ("sbuf", [128, LCOLS], "int32"),
    "negf": ("sbuf", [128, LCOLS], "float32"),
    "rep": ("sbuf", [128, 128], "float32"),
    "ident": ("sbuf", [128, 128], "bfloat16"),
    "idq": ("sbuf", [128, IDW], "bfloat16"),
    "off": ("sbuf", [128, LCOLS], "uint16"),
    "hb": ("sbuf", [128, TOK], "bfloat16"),
    "hp": ("sbuf", [128, TOK], "bfloat16"),
    "mine": ("sbuf", [128, NS], "bfloat16"),
    "pb": ("sbuf", [128, QU], "bfloat16"),
    "relay": ("sbuf", [128, QU], "bfloat16"),
    "lp": ("sbuf", [128, NS], "bfloat16"),
    "la": ("sbuf", [128, NS], "bfloat16"),
    "lb": ("sbuf", [128, NS], "bfloat16"),
    "yo": ("sbuf", [128, NS], "bfloat16"),
    "acc0": ("psum", [128, 512], "float32"),
    "acc1": ("psum", [128, 512], "float32"),
    "acc2": ("psum", [128, 512], "float32"),
    "acc3": ("psum", [128, 512], "float32"),
    "pacc": ("psum", [128, 512], "float32"),
    "offp": ("psum", [128, 512], "float32"),
}
SEMAPHORES = ["stab", "sneg", "sh", "spad", "sone", "srep", "sid", "soff", "scop", "sg0", "sg1", "sent", "arr",
              "rh", "rp", "rs", "rq0", "rq1", "rq2", "rq3", "sp", "spv", "sm0", "sm1", "sm2", "sm3", "sev0", "sev1", "sst"]


def _bits(mask):
    return [e for e in range(mask.bit_length()) if (mask >> e) & 1]


def _engines(mask):
    return len(_bits(mask))


def _pick(mask, i, n):
    return sum(1 << e for e in _bits(mask)[i::n])


def _routes(T, topo):
    out = {}
    n = topo.CORES_PER_CHIP
    for c in T.cores:
        chipmates = [k for k in range(max(0, c - n + 1), c + n)
                     if k not in T.cores and topo.host(k) == topo.host(c) and topo.chip(k) == topo.chip(c)]
        direct = [q for q in T.cores if q != c and topo.may_write(c, q)]
        far = [q for q in T.cores if q != c and not topo.may_write(c, q)]
        far.sort(key=lambda q: topo.host(q) != topo.host(c))

        def in_turn(cores):
            same = [k for k in cores if topo.die(k) == topo.die(c)]
            other = [k for k in cores if topo.die(k) != topo.die(c)]
            return [k for pair in zip(same, other) for k in pair]

        ported = in_turn([k for k in chipmates if all(topo.may_write(k, q) for q in far)])[:NQ]
        spare = in_turn([k for k in chipmates if k not in ported and topo.may_write(k, direct[0])])[:2]
        carriers = []
        for qu, k in enumerate(ported):
            legs = [(q, "a" if topo.host(q) == topo.host(c) else "b", _pick(topo.mask(k, q), j, len(far)))
                    for j, q in enumerate(far)]
            carriers.append((k, qu, _pick(topo.mask(c, k), qu % 2, 2), legs))
        for i, k in enumerate(spare):
            carriers.append((k, NQ - 2 + i, _pick(topo.mask(c, k), i, 2), [(direct[0], "p", topo.mask(k, direct[0]))]))
        out[c] = (direct, carriers)
    return out


def _write(g, topo, src, dst, out_ap, in_ap, remote_sem, local_sem, mask=None):
    rid, pid = topo.addr(dst, src)
    if mask is None:
        mask = topo.mask(src, dst)
    g.remote_dma(out_ap=out_ap, in_ap=in_ap, remote_sem=remote_sem, local_sem=local_sem, pid=pid, routing_id=rid,
                 dma_engine_mask=mask)
    return _engines(mask)


def rank_program(g, core, T, topo):
    sem = T.sem
    routes = _routes(T, topo)
    rank = T.rank_of(core)

    if rank is None:
        for c in T.cores:
            carriers = routes[c][1]
            for i, (k, qu, on, legs) in enumerate(carriers):
                if k != core:
                    continue
                lo, hi = TOK * i // len(carriers), TOK * (i + 1) // len(carriers)
                g.vector.memset(T.idq[:, 0:hi - lo], 1.0).then_inc(sem.sone, 1)
                g.wait_ge(sem.sone, 1)
                g.affine_select(out=T.idq[:, 0:hi - lo], in_=T.idq[:, 0:hi - lo], pattern=[[-1, hi - lo]],
                                compare_op=AluOpType.is_equal, fill=0.0, base=-lo, channel_multiplier=1).then_inc(sem.srep, 1)
                g.wait_ge(sem.srep, 1)
                later = 0
                for q, slot, off in legs:
                    later |= off
                left = _write(g, topo, core, c, T.ident[:, lo:hi], T.idq[:, 0:hi - lo], sem.sid, sem.sent, later)
                g.wait_ge(sem.arr, _engines(on))
                transfers = []
                for q, slot, off in legs:
                    rid, pid = topo.addr(q, core)
                    transfers.append(RemoteDMATransfer(dst_ids=[DstId(rid=rid, pnc=pid)], dma_engine_mask=off,
                                                       remote_sem=sem["rq%d" % qu], src=T.relay[:, :],
                                                       dst=T["l" + slot][:, QU * qu:QU * (qu + 1)]))
                    left += _engines(off)
                g.remote_dma_fused(transfers, local_sem=sem.sent)
                g.wait_ge(sem.sent, left)
        return

    direct, carriers = routes[core]
    partner = direct[0]
    from_partner = _engines(topo.mask(partner, core))
    v, s, sy, pe = g.vector, g.scalar, g.sync, g.tensor
    copy = ActivationFunctionType.Copy

    def quarter(qu):
        return slice(QU * qu, QU * (qu + 1))

    def load_tab(q, p0, p1):
        q.dma_start(T.win[p0:p1, PAD:PAD + ITEMS], T.tab[p0:p1, :]).then_inc(sem.stab, 16)

    sy.dma_start(T.negs[0:GROUP, :], T.neg[:, :]).then_inc(sem.sneg, 16)
    s.dma_start(T.hb[:, :], T.h[:, :]).then_inc(sem.sh, 16)
    load_tab(s, 32, 64)
    load_tab(sy, 0, 32)
    load_tab(s, 96, 128)
    load_tab(sy, 64, 96)

    v.memset(T.rep[0:GROUP, :], 1.0).then_inc(sem.sone, 1)
    v.memset(T.win[:, 0:PAD], 0.0).then_inc(sem.spad, 1)
    v.memset(T.win[:, PAD + ITEMS:WIN], 0.0).then_inc(sem.spad, 1)
    g.wait_ge(sem.sone, 1)
    g.affine_select(out=T.rep[0:GROUP, :], in_=T.rep[0:GROUP, :], pattern=[[0, 128 // GROUP], [-1, GROUP]],
                    compare_op=AluOpType.is_equal, fill=0.0, base=0, channel_multiplier=1).then_inc(sem.srep, 1)
    g.wait_ge(sem.sh, 16)
    left = _write(g, topo, core, partner, T.hp[:, :], T.hb[:, :], sem.rh, sem.sent)

    v.wait_ge(sem.sneg, 16)
    v.tensor_scalar(out=T.negf[0:GROUP, :], in0=T.negs[0:GROUP, :], scalar1=PAD - ITEMS * rank, scalar2=0,
                    op0=AluOpType.add, op1=AluOpType.max).then_inc(sem.soff, 1)
    pe.wait_ge(sem.srep, 1)
    pe.wait_ge(sem.soff, 1)
    pe.matmul(T.offp[:, 0:LCOLS], T.rep[0:GROUP, :], T.negf[0:GROUP, :], True, True).then_inc(sem.scop, 1)
    v.wait_ge(sem.scop, 1)
    v.tensor_scalar(out=T.off[:, :], in0=T.offp[:, 0:LCOLS], scalar1=PAD + ITEMS, scalar2=None,
                    op0=AluOpType.min).then_inc(sem.soff, 1)

    for q in (v, s):
        q.wait_ge(sem.soff, 2)
        q.wait_ge(sem.spad, 2)
        q.wait_ge(sem.stab, 64)
    lq = LCOLS // NQ
    for ch in range(2):
        q0, q1 = 2 * ch, 2 * ch + 1
        v.tensor_copy(out=T.mine[:, quarter(q0)],
                      in_=T.win[:, 0:WIN].indirect(T.off[:, lq * q0:lq * (q0 + 1)])).then_inc(sem["sg%d" % ch], 1)
        s.activation(out=T.mine[:, quarter(q1)],
                     in_=T.win[:, 0:WIN].indirect(T.off[:, lq * q1:lq * (q1 + 1)]), func=copy).then_inc(sem["sg%d" % ch], 1)

    seen = -1
    for i in range(0, len(carriers), 2):
        transfers = []
        for k, qu, on, legs in carriers[i:i + 2]:
            while seen < qu // 2:
                seen += 1
                g.wait_ge(sem["sg%d" % seen], 2)
            rid, pid = topo.addr(k, core)
            transfers.append(RemoteDMATransfer(dst_ids=[DstId(rid=rid, pnc=pid)], dma_engine_mask=on, remote_sem=sem.arr,
                                               src=T.mine[:, quarter(qu)], dst=T.relay[:, :]))
            left += _engines(on)
        g.remote_dma_fused(transfers, local_sem=sem.sent)
    left += _write(g, topo, core, partner, T.lp[:, quarter(QRAW)], T.mine[:, quarter(QRAW)], sem.rp, sem.sent)
    g.wait_ge(sem.spv, 1)
    left += _write(g, topo, core, partner, T.lp[:, quarter(QSC)], T.pb[:, :], sem.rs, sem.sent)

    def mm(lhsT, buf, qu, first, last):
        m = pe.matmul(T["acc%d" % qu][:, 0:QU], lhsT[:, :], buf[:, quarter(qu)], first, last)
        if last:
            m.then_inc(sem["sm%d" % qu], 1)

    came = {qu: [] for qu in range(NQ)}
    ident_in = 0
    for c in T.cores:
        for k, qu, on, legs in routes[c][1]:
            for q, slot, off in legs:
                if q == core:
                    came[qu].append((slot, _engines(off)))
                if c == core:
                    ident_in += _engines(off)

    def carried(qu):
        pe.wait_ge(sem["rq%d" % qu], sum(n for slot, n in came[qu]))
        slots = sorted(slot for slot, n in came[qu])
        for slot in slots:
            mm(T.hb, T["l" + slot], qu, False, slot == slots[-1])

    pe.wait_ge(sem.sh, 16)
    pe.wait_ge(sem.sg0, 2)
    mm(T.hb, T.mine, 0, True, False)
    mm(T.hb, T.mine, 1, True, False)
    pe.wait_ge(sem.rh, from_partner)
    pe.matmul(T.pacc[:, 0:QU], T.hp[:, :], T.mine[:, quarter(QSC)], True, True).then_inc(sem.sp, 1)
    pe.wait_ge(sem.sg1, 2)
    mm(T.hb, T.mine, 2, True, False)
    mm(T.hb, T.mine, 3, True, False)
    pe.wait_ge(sem.rp, from_partner)
    mm(T.hb, T.lp, QRAW, False, False)
    carried(QRAW)
    pe.wait_ge(sem.sid, ident_in)
    pe.wait_ge(sem.rs, from_partner)
    mm(T.ident, T.lp, QSC, False, False)
    carried(QSC)
    carried(2)
    carried(3)

    v.wait_ge(sem.sp, 1)
    v.tensor_copy(out=T.pb[:, :], in_=T.pacc[:, 0:QU]).then_inc(sem.spv, 1)

    for ch in range(2):
        q0, q1 = 2 * ch, 2 * ch + 1
        v.wait_ge(sem["sm%d" % q0], 1)
        v.tensor_copy(out=T.yo[:, quarter(q0)], in_=T["acc%d" % q0][:, 0:QU]).then_inc(sem["sev%d" % ch], 1)
        s.wait_ge(sem["sm%d" % q1], 1)
        s.activation(out=T.yo[:, quarter(q1)], in_=T["acc%d" % q1][:, 0:QU],
                     func=copy).then_inc(sem["sev%d" % ch], 1)
        cols = slice(CH * ch, CH * (ch + 1))
        sy.wait_ge(sem["sev%d" % ch], 2)
        sy.dma_start(T.y[:, cols], T.yo[:, cols]).then_inc(sem.sst, 16)
    sy.wait_ge(sem.sst, 32)
    g.wait_ge(sem.sent, left)
